import numpy as np
import ml_dtypes


def mxq(x, axis, fmt="e4m3"):
    dtype, down = {"e4m3": (ml_dtypes.float8_e4m3fn, 7), "e5m2": (ml_dtypes.float8_e5m2, 14)}[fmt]
    v = np.moveaxis(np.asarray(x, np.float32).astype(ml_dtypes.bfloat16).astype(np.float64), axis, -1)
    blocks = v.reshape(v.shape[:-1] + (-1, 32))
    amax = np.abs(blocks).max(-1, keepdims=True)
    byte = np.maximum(np.where(amax > 0, np.frexp(amax)[1] - 1 + 127, 0) - down, 1)
    scale = np.exp2(byte - 127.0)
    codes = (blocks / scale).astype(np.float32).astype(dtype).astype(np.float64)
    return np.moveaxis((codes * scale).reshape(v.shape), -1, axis)


WIDE = False


def mx_kscale(k):
    if not WIDE:
        return np.ones(k)
    levels = np.array([10, -10, 5, -5, 0])
    if k % 512:
        return np.exp2(np.random.permutation(np.resize(levels, k // 32))).repeat(32)
    a = np.empty((k // 512, 16))
    for p in range(k // 512):
        a[p, :8] = np.random.permutation(np.resize(levels, 8))
        for g in range(8):
            far = levels[np.abs(levels - a[p, g]) >= 10]
            a[p, g + 8] = far[np.random.randint(len(far))]
    return np.exp2(a.ravel()).repeat(32)


def f64(x):
    return np.asarray(x).astype(np.float64)


def striped(idx):
    return np.tile(np.asarray(idx).reshape(-1, 16).T, (8, 1)).astype(np.uint16)


def unstriped(offs):
    return offs[:16].T.reshape(-1).astype(np.int64)


G, T, T2, D, M = 256, 1024, 1024, 1024, 256


def setup_inputs():
    n = np.random.standard_normal
    s = mx_kscale(D)[:, None]
    return {
        "xT": (n((D, T)) * s).astype(np.float32),
        "w": (n((D, M)) / np.sqrt(D) / s).astype(np.float32),
        "cache": n((M, T2)).astype(np.float32),
        "bias": (0.3 * n((M, 1))).astype(np.float32),
        "offs": striped(np.random.permutation(T)[:G]),
        "slots": striped(np.random.permutation(T2)[:G]),
    }


def reference(xT, w, cache, bias, offs, slots):
    y = mxq(f64(w), 0, "e4m3").T @ mxq(f64(xT)[:, unstriped(offs)], 0, "e4m3")
    y = y + f64(bias)
    out = f64(cache).copy()
    out[:, unstriped(slots)] = y
    return out

@@ -1,0 +1,109 @@
+from contextlib import ExitStack
+
+import concourse.mybir as mybir
+
+F32 = mybir.dt.float32
+BF16 = mybir.dt.bfloat16
+U32 = mybir.dt.uint32
+U16 = mybir.dt.uint16
+U8 = mybir.dt.uint8
+FP8X4 = mybir.dt.float8_e4m3fn_x4
+COPY = mybir.ActivationFunctionType.Copy
+IDENTITY = mybir.ActivationFunctionType.Identity
+
+P = 128
+PACK = 4
+G, T, T2, D, M = 256, 1024, 1024, 1024, 256
+PASSES = D // (P * PACK)
+BLOCKS = M // P
+
+FLOPS = 2 * D * M * G
+
+
+def tile_attend_fill_bias_kernel(tc, xT, w, cache, bias, offs, slots, out):
+    nc = tc.nc
+    x_rows = xT.rearrange("(g p j) n -> g p j n", p=P, j=PACK)
+    w_rows = w.rearrange("(g p j) m -> g p j m", p=P, j=PACK)
+    cache_rows = cache.rearrange("(p t) n -> t p n", t=BLOCKS)
+    out_rows = out.rearrange("(p t) n -> t p n", t=BLOCKS)
+
+    with ExitStack() as ctx:
+        lists = ctx.enter_context(tc.tile_pool(name="lists", bufs=1))
+        keep = ctx.enter_context(tc.tile_pool(name="keep", bufs=1))
+        psum = ctx.enter_context(tc.psum_pool(name="psum", bufs=1))
+
+        offs_sb = lists.tile([P, G // 16], U16, name="offs_sb")
+        nc.sync.dma_start(offs_sb[:], offs)
+        bias_sb = keep.tile([P, BLOCKS], F32, name="bias_sb")
+        nc.scalar.dma_start(out=bias_sb[:], in_=bias.rearrange("(p t) o -> p (t o)", t=BLOCKS))
+
+        x_sb = {}
+        w_sb = []
+
+        def load_x(g, j0, count):
+            rows = keep.tile([P, count, T], F32, name=f"x_{g}_{j0}")
+            nc.sync.dma_start(out=rows[:], in_=x_rows[g, :, j0 : j0 + count, :])
+            for j in range(count):
+                x_sb[g, j0 + j] = rows[:, j, :]
+
+        def load_w(g):
+            rows = keep.tile([P, PACK, M], F32, name=f"w_{g}")
+            nc.sync.dma_start(out=rows[:], in_=w_rows[g])
+            w_sb.append(rows)
+
+        load_x(0, 0, 2)
+        load_x(0, 2, 2)
+        load_w(0)
+        load_w(1)
+        load_x(1, 0, 2)
+        load_x(1, 2, 1)
+        load_x(1, 3, 1)
+        slots_sb = lists.tile([P, G // 16], U16, name="slots_sb")
+        nc.sync.dma_start(slots_sb[:], slots)
+        cache_sb = []
+        for t in range(BLOCKS):
+            rows = keep.tile([P, T2], F32, name=f"cache_{t}")
+            nc.sync.dma_start(out=rows[:], in_=cache_rows[t])
+            cache_sb.append(rows)
+
+        acc = [psum.tile([P, G], F32, name=f"acc_{t}") for t in range(BLOCKS)]
+
+        def quantize(name, grouped, width):
+            codes = keep.tile([P, width], U32, name=f"{name}_codes", align_bytes=64)
+            scales = keep.tile([P, width], U8, name=f"{name}_scales", align_bytes=64)
+            nc.vector.quantize_mx(
+                out=codes[:].bitcast(FP8X4),
+                scales=scales[:],
+                in_=grouped[:].rearrange("p n j -> p (n j)"),
+            )
+            return codes, scales
+
+        for g in range(PASSES):
+            w_grouped = keep.tile([P, M, PACK], BF16, name=f"w_grouped_{g}", align_bytes=64)
+            nc.scalar.activation(
+                w_grouped[:].rearrange("p (t m) j -> p t m j", t=BLOCKS),
+                w_sb[g][:].rearrange("p j (m t) -> p t m j", t=BLOCKS),
+                COPY,
+            )
+            x_grouped = keep.tile([P, G, PACK], BF16, name=f"x_grouped_{g}", align_bytes=64)
+            for j in range(PACK):
+                nc.vector.tensor_copy(out=x_grouped[:, :, j], in_=x_sb[g, j].indirect(offs_sb[:]))
+            w_codes, w_scales = quantize(f"w{g}", w_grouped, M)
+            x_codes, x_scales = quantize(f"x{g}", x_grouped, G)
+            for t in range(BLOCKS):
+                columns = slice(t * P, (t + 1) * P)
+                nc.tensor.matmul_mx(
+                    out=acc[t][:],
+                    lhsT=w_codes[:, columns].bitcast(FP8X4),
+                    lhsT_scale=w_scales[:, columns],
+                    rhs=x_codes[:].bitcast(FP8X4),
+                    rhs_scale=x_scales[:],
+                    start=(g == 0),
+                    stop=(g == PASSES - 1),
+                )
+
+        for t in range(BLOCKS):
+            y = keep.tile([P, G], F32, name=f"y_{t}")
+            nc.scalar.activation(y[:], acc[t][:], IDENTITY, bias=bias_sb[:, t : t + 1])
+            nc.vector.tensor_copy(out=cache_sb[t][:].indirect(slots_sb[:]), in_=y[:])
+            nc.sync.dma_start(out=out_rows[t], in_=cache_sb[t][:])

@@ -34,9 +34,6 @@ def tile_attend_fill_bias_kernel(tc, xT, w, cache, bias, offs, slots, out):
 
         offs_sb = lists.tile([P, G // 16], U16, name="offs_sb")
         nc.sync.dma_start(offs_sb[:], offs)
-        bias_sb = keep.tile([P, BLOCKS], F32, name="bias_sb")
-        nc.scalar.dma_start(out=bias_sb[:], in_=bias.rearrange("(p t) o -> p (t o)", t=BLOCKS))
-
         x_sb = {}
         w_sb = []
 
@@ -53,20 +50,20 @@ def tile_attend_fill_bias_kernel(tc, xT, w, cache, bias, offs, slots, out):
 
         load_x(0, 0, 2)
         load_x(0, 2, 2)
-        load_w(0)
-        load_w(1)
         load_x(1, 0, 2)
         load_x(1, 2, 1)
         load_x(1, 3, 1)
+        load_w(0)
+        load_w(1)
         slots_sb = lists.tile([P, G // 16], U16, name="slots_sb")
         nc.sync.dma_start(slots_sb[:], slots)
+        bias_sb = keep.tile([P, BLOCKS], F32, name="bias_sb")
+        nc.sync.dma_start(out=bias_sb[:], in_=bias.rearrange("(p t) o -> p (t o)", t=BLOCKS))
         cache_sb = []
         for t in range(BLOCKS):
             rows = keep.tile([P, T2], F32, name=f"cache_{t}")
             nc.sync.dma_start(out=rows[:], in_=cache_rows[t])
             cache_sb.append(rows)
-
-        acc = [psum.tile([P, G], F32, name=f"acc_{t}") for t in range(BLOCKS)]
 
         def quantize(name, grouped, width):
             codes = keep.tile([P, width], U32, name=f"{name}_codes", align_bytes=64)
@@ -78,32 +75,61 @@ def tile_attend_fill_bias_kernel(tc, xT, w, cache, bias, offs, slots, out):
             )
             return codes, scales
 
-        for g in range(PASSES):
-            w_grouped = keep.tile([P, M, PACK], BF16, name=f"w_grouped_{g}", align_bytes=64)
-            nc.scalar.activation(
-                w_grouped[:].rearrange("p (t m) j -> p t m j", t=BLOCKS),
-                w_sb[g][:].rearrange("p j (m t) -> p t m j", t=BLOCKS),
-                COPY,
-            )
+        x_mx, w_mx = [], {}
+
+        def gather(g):
             x_grouped = keep.tile([P, G, PACK], BF16, name=f"x_grouped_{g}", align_bytes=64)
             for j in range(PACK):
                 nc.vector.tensor_copy(out=x_grouped[:, :, j], in_=x_sb[g, j].indirect(offs_sb[:]))
-            w_codes, w_scales = quantize(f"w{g}", w_grouped, M)
-            x_codes, x_scales = quantize(f"x{g}", x_grouped, G)
-            for t in range(BLOCKS):
-                columns = slice(t * P, (t + 1) * P)
-                nc.tensor.matmul_mx(
-                    out=acc[t][:],
-                    lhsT=w_codes[:, columns].bitcast(FP8X4),
-                    lhsT_scale=w_scales[:, columns],
-                    rhs=x_codes[:].bitcast(FP8X4),
-                    rhs_scale=x_scales[:],
-                    start=(g == 0),
-                    stop=(g == PASSES - 1),
-                )
+            return x_grouped
 
+        def interleave(g, t, parts):
+            w_grouped = keep.tile([P, P, PACK], BF16, name=f"w_grouped_{g}_{t}", align_bytes=64)
+            source = w_sb[g][:].rearrange("p j (m t) -> p t m j", t=BLOCKS)[:, t]
+            for engine, m0, m1 in parts:
+                if engine == "scalar":
+                    nc.scalar.activation(w_grouped[:, m0:m1, :], source[:, m0:m1, :], COPY)
+                else:
+                    nc.vector.tensor_copy(out=w_grouped[:, m0:m1, :], in_=source[:, m0:m1, :])
+            return w_grouped
+
+        pieces = [(0, 0, G), (1, 0, G)]
+        acc = [psum.tile([P, n1 - n0], F32, name=f"acc_{t}_{n0}") for t, n0, n1 in pieces]
+
+        def multiply(g, t):
+            w_codes, w_scales = w_mx[g, t]
+            x_codes, x_scales = x_mx[g]
+            for i, (block, n0, n1) in enumerate(pieces):
+                if block == t:
+                    nc.tensor.matmul_mx(
+                        out=acc[i][:],
+                        lhsT=w_codes[:].bitcast(FP8X4),
+                        lhsT_scale=w_scales[:],
+                        rhs=x_codes[:, n0:n1].bitcast(FP8X4),
+                        rhs_scale=x_scales[:, n0:n1],
+                        start=(g == 0),
+                        stop=(g == PASSES - 1),
+                    )
+
+        x0 = gather(0)
+        x_mx.append(quantize("x0", x0, G))
+        x1 = gather(1)
+        x_mx.append(quantize("x1", x1, G))
+        wg = {}
         for t in range(BLOCKS):
-            y = keep.tile([P, G], F32, name=f"y_{t}")
-            nc.scalar.activation(y[:], acc[t][:], IDENTITY, bias=bias_sb[:, t : t + 1])
-            nc.vector.tensor_copy(out=cache_sb[t][:].indirect(slots_sb[:]), in_=y[:])
-            nc.sync.dma_start(out=out_rows[t], in_=cache_sb[t][:])
+            wg[0, t] = interleave(0, t, [("vector" if t == 0 else "scalar", 0, P)])
+        for t in range(BLOCKS):
+            w_mx[0, t] = quantize(f"w0{t}", wg[0, t], P)
+            multiply(0, t)
+        wg[1, 0] = interleave(1, 0, [("vector", 0, P)])
+        wg[1, 1] = interleave(1, 1, [("scalar", 0, P)])
+        for t in range(BLOCKS):
+            w_mx[1, t] = quantize(f"w1{t}", wg[1, t], P)
+            multiply(1, t)
+
+        for i, (t, n0, n1) in enumerate(pieces):
+            y = keep.tile([P, n1 - n0], F32, name=f"y_{t}_{n0}")
+            nc.scalar.activation(y[:], acc[i][:], IDENTITY, bias=bias_sb[:, t : t + 1])
+            nc.vector.tensor_copy(out=cache_sb[t][:].indirect(slots_sb[:, n0 // 16 : n1 // 16]), in_=y[:])
+            if n1 == G:
+                nc.sync.dma_start(out=out_rows[t], in_=cache_sb[t][:])

@@ -50,9 +50,8 @@ def tile_attend_fill_bias_kernel(tc, xT, w, cache, bias, offs, slots, out):
 
         load_x(0, 0, 2)
         load_x(0, 2, 2)
-        load_x(1, 0, 2)
-        load_x(1, 2, 1)
-        load_x(1, 3, 1)
+        for j in range(PACK):
+            load_x(1, j, 1)
         load_w(0)
         load_w(1)
         slots_sb = lists.tile([P, G // 16], U16, name="slots_sb")
@@ -87,10 +86,12 @@ def tile_attend_fill_bias_kernel(tc, xT, w, cache, bias, offs, slots, out):
             w_grouped = keep.tile([P, P, PACK], BF16, name=f"w_grouped_{g}_{t}", align_bytes=64)
             source = w_sb[g][:].rearrange("p j (m t) -> p t m j", t=BLOCKS)[:, t]
             for engine, m0, m1 in parts:
+                target = w_grouped[:, m0:m1, :].rearrange("p (c i) j -> p c j i", i=4)
+                rows = source[:, m0:m1, :].rearrange("p (c i) j -> p c j i", i=4)
                 if engine == "scalar":
-                    nc.scalar.activation(w_grouped[:, m0:m1, :], source[:, m0:m1, :], COPY)
+                    nc.scalar.activation(target, rows, COPY)
                 else:
-                    nc.vector.tensor_copy(out=w_grouped[:, m0:m1, :], in_=source[:, m0:m1, :])
+                    nc.vector.tensor_copy(out=target, in_=rows)
             return w_grouped
 
         pieces = [(0, 0, G), (1, 0, G)]

@@ -94,7 +94,7 @@ def tile_attend_fill_bias_kernel(tc, xT, w, cache, bias, offs, slots, out):
                     nc.vector.tensor_copy(out=target, in_=rows)
             return w_grouped
 
-        pieces = [(0, 0, G), (1, 0, G)]
+        pieces = [(0, 0, G // 2), (0, G // 2, G), (1, 0, G)]
         acc = [psum.tile([P, n1 - n0], F32, name=f"acc_{t}_{n0}") for t, n0, n1 in pieces]
 
         def multiply(g, t):
@@ -122,15 +122,16 @@ def tile_attend_fill_bias_kernel(tc, xT, w, cache, bias, offs, slots, out):
         for t in range(BLOCKS):
             w_mx[0, t] = quantize(f"w0{t}", wg[0, t], P)
             multiply(0, t)
-        wg[1, 0] = interleave(1, 0, [("vector", 0, P)])
+        wg[1, 0] = interleave(1, 0, [("scalar", 0, P // 2), ("vector", P // 2, P)])
         wg[1, 1] = interleave(1, 1, [("scalar", 0, P)])
         for t in range(BLOCKS):
             w_mx[1, t] = quantize(f"w1{t}", wg[1, t], P)
             multiply(1, t)
 
-        for i, (t, n0, n1) in enumerate(pieces):
-            y = keep.tile([P, n1 - n0], F32, name=f"y_{t}_{n0}")
-            nc.scalar.activation(y[:], acc[i][:], IDENTITY, bias=bias_sb[:, t : t + 1])
-            nc.vector.tensor_copy(out=cache_sb[t][:].indirect(slots_sb[:, n0 // 16 : n1 // 16]), in_=y[:])
-            if n1 == G:
-                nc.sync.dma_start(out=out_rows[t], in_=cache_sb[t][:])
+        for t in range(BLOCKS):
+            y = keep.tile([P, G], F32, name=f"y_{t}")
+            for i, (block, n0, n1) in enumerate(pieces):
+                if block == t:
+                    nc.scalar.activation(y[:, n0:n1], acc[i][:], IDENTITY, bias=bias_sb[:, t : t + 1])
+            nc.vector.tensor_copy(out=cache_sb[t][:].indirect(slots_sb[:]), in_=y[:])
+            nc.sync.dma_start(out=out_rows[t], in_=cache_sb[t][:])

from contextlib import ExitStack

import concourse.mybir as mybir

F32 = mybir.dt.float32
BF16 = mybir.dt.bfloat16
U32 = mybir.dt.uint32
U16 = mybir.dt.uint16
U8 = mybir.dt.uint8
FP8X4 = mybir.dt.float8_e4m3fn_x4
COPY = mybir.ActivationFunctionType.Copy
IDENTITY = mybir.ActivationFunctionType.Identity

P = 128
PACK = 4
G, T, T2, D, M = 256, 1024, 1024, 1024, 256
PASSES = D // (P * PACK)
BLOCKS = M // P

FLOPS = 2 * D * M * G


def tile_attend_fill_bias_kernel(tc, xT, w, cache, bias, offs, slots, out):
    nc = tc.nc
    x_rows = xT.rearrange("(g p j) n -> g p j n", p=P, j=PACK)
    w_rows = w.rearrange("(g p j) m -> g p j m", p=P, j=PACK)
    cache_rows = cache.rearrange("(p t) n -> t p n", t=BLOCKS)
    out_rows = out.rearrange("(p t) n -> t p n", t=BLOCKS)

    with ExitStack() as ctx:
        lists = ctx.enter_context(tc.tile_pool(name="lists", bufs=1))
        keep = ctx.enter_context(tc.tile_pool(name="keep", bufs=1))
        psum = ctx.enter_context(tc.psum_pool(name="psum", bufs=1))

        offs_sb = lists.tile([P, G // 16], U16, name="offs_sb")
        nc.sync.dma_start(offs_sb[:], offs)
        x_sb = {}
        w_sb = []

        def load_x(g, j0, count):
            rows = keep.tile([P, count, T], F32, name=f"x_{g}_{j0}")
            nc.sync.dma_start(out=rows[:], in_=x_rows[g, :, j0 : j0 + count, :])
            for j in range(count):
                x_sb[g, j0 + j] = rows[:, j, :]

        def load_w(g):
            rows = keep.tile([P, PACK, M], F32, name=f"w_{g}")
            nc.sync.dma_start(out=rows[:], in_=w_rows[g])
            w_sb.append(rows)

        load_x(0, 0, 2)
        load_x(0, 2, 2)
        for j in range(PACK):
            load_x(1, j, 1)
        load_w(0)
        load_w(1)
        slots_sb = lists.tile([P, G // 16], U16, name="slots_sb")
        nc.sync.dma_start(slots_sb[:], slots)
        bias_sb = keep.tile([P, BLOCKS], F32, name="bias_sb")
        nc.sync.dma_start(out=bias_sb[:], in_=bias.rearrange("(p t) o -> p (t o)", t=BLOCKS))
        cache_sb = []
        for t in range(BLOCKS):
            rows = keep.tile([P, T2], F32, name=f"cache_{t}")
            nc.sync.dma_start(out=rows[:], in_=cache_rows[t])
            cache_sb.append(rows)

        def quantize(name, grouped, width):
            codes = keep.tile([P, width], U32, name=f"{name}_codes", align_bytes=64)
            scales = keep.tile([P, width], U8, name=f"{name}_scales", align_bytes=64)
            nc.vector.quantize_mx(
                out=codes[:].bitcast(FP8X4),
                scales=scales[:],
                in_=grouped[:].rearrange("p n j -> p (n j)"),
            )
            return codes, scales

        x_mx, w_mx = [], {}

        def gather(g):
            x_grouped = keep.tile([P, G, PACK], BF16, name=f"x_grouped_{g}", align_bytes=64)
            for j in range(PACK):
                nc.vector.tensor_copy(out=x_grouped[:, :, j], in_=x_sb[g, j].indirect(offs_sb[:]))
            return x_grouped

        def interleave(g, t, parts):
            w_grouped = keep.tile([P, P, PACK], BF16, name=f"w_grouped_{g}_{t}", align_bytes=64)
            source = w_sb[g][:].rearrange("p j (m t) -> p t m j", t=BLOCKS)[:, t]
            for engine, m0, m1 in parts:
                target = w_grouped[:, m0:m1, :].rearrange("p (c i) j -> p c j i", i=4)
                rows = source[:, m0:m1, :].rearrange("p (c i) j -> p c j i", i=4)
                if engine == "scalar":
                    nc.scalar.activation(target, rows, COPY)
                else:
                    nc.vector.tensor_copy(out=target, in_=rows)
            return w_grouped

        pieces = [(0, 0, G // 2), (0, G // 2, G), (1, 0, G)]
        acc = [psum.tile([P, n1 - n0], F32, name=f"acc_{t}_{n0}") for t, n0, n1 in pieces]

        def multiply(g, t):
            w_codes, w_scales = w_mx[g, t]
            x_codes, x_scales = x_mx[g]
            for i, (block, n0, n1) in enumerate(pieces):
                if block == t:
                    nc.tensor.matmul_mx(
                        out=acc[i][:],
                        lhsT=w_codes[:].bitcast(FP8X4),
                        lhsT_scale=w_scales[:],
                        rhs=x_codes[:, n0:n1].bitcast(FP8X4),
                        rhs_scale=x_scales[:, n0:n1],
                        start=(g == 0),
                        stop=(g == PASSES - 1),
                    )

        x0 = gather(0)
        x_mx.append(quantize("x0", x0, G))
        x1 = gather(1)
        x_mx.append(quantize("x1", x1, G))
        wg = {}
        for t in range(BLOCKS):
            wg[0, t] = interleave(0, t, [("vector" if t == 0 else "scalar", 0, P)])
        for t in range(BLOCKS):
            w_mx[0, t] = quantize(f"w0{t}", wg[0, t], P)
            multiply(0, t)
        wg[1, 0] = interleave(1, 0, [("scalar", 0, P // 2), ("vector", P // 2, P)])
        wg[1, 1] = interleave(1, 1, [("scalar", 0, P)])
        for t in range(BLOCKS):
            w_mx[1, t] = quantize(f"w1{t}", wg[1, t], P)
            multiply(1, t)

        for t in range(BLOCKS):
            y = keep.tile([P, G], F32, name=f"y_{t}")
            for i, (block, n0, n1) in enumerate(pieces):
                if block == t:
                    nc.scalar.activation(y[:, n0:n1], acc[i][:], IDENTITY, bias=bias_sb[:, t : t + 1])
            nc.vector.tensor_copy(out=cache_sb[t][:].indirect(slots_sb[:]), in_=y[:])
            nc.sync.dma_start(out=out_rows[t], in_=cache_sb[t][:])
